import numpy as np
import ml_dtypes


def mxq(x, axis, fmt="e4m3"):
    dtype, down = {"e4m3": (ml_dtypes.float8_e4m3fn, 7), "e5m2": (ml_dtypes.float8_e5m2, 14)}[fmt]
    v = np.moveaxis(np.asarray(x, np.float32).astype(ml_dtypes.bfloat16).astype(np.float64), axis, -1)
    blocks = v.reshape(v.shape[:-1] + (-1, 32))
    amax = np.abs(blocks).max(-1, keepdims=True)
    byte = np.maximum(np.where(amax > 0, np.frexp(amax)[1] - 1 + 127, 0) - down, 1)
    scale = np.exp2(byte - 127.0)
    codes = (blocks / scale).astype(np.float32).astype(dtype).astype(np.float64)
    return np.moveaxis((codes * scale).reshape(v.shape), -1, axis)


WIDE = False


def mx_kscale(k):
    if not WIDE:
        return np.ones(k)
    levels = np.array([10, -10, 5, -5, 0])
    if k % 512:
        return np.exp2(np.random.permutation(np.resize(levels, k // 32))).repeat(32)
    a = np.empty((k // 512, 16))
    for p in range(k // 512):
        a[p, :8] = np.random.permutation(np.resize(levels, 8))
        for g in range(8):
            far = levels[np.abs(levels - a[p, g]) >= 10]
            a[p, g + 8] = far[np.random.randint(len(far))]
    return np.exp2(a.ravel()).repeat(32)


def f64(x):
    return np.asarray(x).astype(np.float64)


def striped(idx):
    return np.tile(idx.reshape(-1, 16).T, (8, 1)).astype(np.uint16)


def unstriped(offs):
    return offs[:16].T.reshape(-1).astype(np.int64)


E2M1 = np.array([0.0, 0.5, 1.0, 1.5, 2.0, 3.0, 4.0, 6.0, -0.0, -0.5, -1.0, -1.5, -2.0, -3.0, -4.0, -6.0])


def pack_weight(w, fmt):
    k, n = w.shape
    w = f64(np.asarray(w, np.float32).astype(ml_dtypes.bfloat16)).reshape(k // 32, 32, n)
    amax = np.abs(w).max(1)
    if fmt == "e4m3":
        byte = np.frexp(amax)[1] - 1 + 127 - 7
    else:
        mant, ex = np.frexp(amax / 6.0)
        byte = np.where(mant > 0.5, ex, ex - 1) + 127
    byte = np.clip(np.where(amax > 0, byte, 1), 1, 254)
    scaled = (w * np.exp2(127.0 - byte)[:, None, :]).reshape(k, n).astype(np.float32)
    by_word = np.ascontiguousarray(scaled.reshape(k // 512, 128, 4, n).transpose(0, 1, 3, 2))
    if fmt == "e4m3":
        words = by_word.astype(ml_dtypes.float8_e4m3fn).view(np.uint8)
    else:
        c = by_word.astype(ml_dtypes.float4_e2m1fn).view(np.uint8) & 0xF
        words = (c[..., 0::2] | (c[..., 1::2] << 4)).reshape(k // 512, 128, 2 * n)
    return np.ascontiguousarray(words), np.ascontiguousarray(byte.astype(np.uint8).reshape(k // 512, 16, n))


def unpack_weight(words, scales, fmt):
    g, _, n = scales.shape
    words = np.ascontiguousarray(words).reshape(g, 128, n, -1)
    if fmt == "e4m3":
        vals = words.view(ml_dtypes.float8_e4m3fn).astype(np.float64)
    else:
        nib = np.empty((g, 128, n, 4), np.uint8)
        nib[..., 0::2] = words & 0xF
        nib[..., 1::2] = words >> 4
        vals = E2M1[nib]
    vals = vals * np.repeat(np.exp2(scales.astype(np.float64) - 127.0), 8, axis=1)[..., None]
    return vals.transpose(0, 1, 3, 2).reshape(g * 512, n)


def relu(v):
    return np.maximum(v, 0.0)


K, T, E, C, H, N = 512, 1280, 4, 256, 512, 384


def by_expert(wq, xq):
    return np.concatenate([wq[e].T @ xq[:, e * C:(e + 1) * C] for e in range(E)], axis=1)


def setup_inputs():
    n = np.random.standard_normal
    s = mx_kscale(K)[:, None]
    u = mx_kscale(H)
    w1 = [pack_weight(m, "e2m1") for m in n((E, K, H)) / np.sqrt(K) / s[None]]
    w3 = [pack_weight(m, "e2m1") for m in n((E, K, H)) / np.sqrt(K) / s[None] * u[None, None, :]]
    w2 = [pack_weight(m, "e2m1") for m in n((E, H, N)) / np.sqrt(H) / u[None, :, None]]
    x = pack_weight(n((K, T)) * s, "e4m3")
    return {
        "x_words": x[0],
        "x_scales": x[1],
        "w1_words": np.stack([m[0] for m in w1]),
        "w1_scales": np.stack([m[1] for m in w1]),
        "w3_words": np.stack([m[0] for m in w3]),
        "w3_scales": np.stack([m[1] for m in w3]),
        "w2_words": np.stack([m[0] for m in w2]),
        "w2_scales": np.stack([m[1] for m in w2]),
        "gate": np.tile(np.random.uniform(0.2, 1.0, E * C), (N, 1)).astype(np.float32),
        "offs": striped(np.random.permutation(T)[:E * C]),
    }


def reference(x_words, x_scales, w1_words, w1_scales, w3_words, w3_scales, w2_words, w2_scales, gate, offs):
    idx = unstriped(offs)
    w1 = np.stack([unpack_weight(w1_words[e], w1_scales[e], "e2m1") for e in range(E)])
    w3 = np.stack([unpack_weight(w3_words[e], w3_scales[e], "e2m1") for e in range(E)])
    w2 = np.stack([unpack_weight(w2_words[e], w2_scales[e], "e2m1") for e in range(E)])
    xq = unpack_weight(x_words, x_scales, "e4m3")[:, idx]
    h = relu(by_expert(w1, xq))
    h = h * by_expert(w3, xq)
    y = by_expert(w2, mxq(h, 0, "e4m3"))
    out = np.zeros((N, T))
    out[:, idx] = f64(gate) * y
    return out

@@ -1,0 +1,184 @@
+from contextlib import ExitStack
+
+import concourse.mybir as mybir
+
+K, T, E, C, H, N = 512, 1280, 4, 256, 512, 384
+S = E * C
+P = 128
+FLOPS = 2 * S * (2 * K * H + H * N)
+
+F32 = mybir.dt.float32
+BF16 = mybir.dt.bfloat16
+I32 = mybir.dt.int32
+U32 = mybir.dt.uint32
+U16 = mybir.dt.uint16
+U8 = mybir.dt.uint8
+FP8X4 = mybir.dt.float8_e4m3fn_x4
+FP4X4 = mybir.dt.float4_e2m1fn_x4
+MULT = mybir.AluOpType.mult
+RELU = mybir.ActivationFunctionType.Relu
+
+WIDE = 1376
+
+
+def tile_moe_pkd_glu_relu_kernel(
+    tc, x_words, x_scales, w1_words, w1_scales, w3_words, w3_scales, w2_words, w2_scales, gate, offs, out
+):
+    nc = tc.nc
+    with ExitStack() as ctx:
+        keep = ctx.enter_context(tc.tile_pool(name="keep", bufs=1))
+        ring = ctx.enter_context(tc.tile_pool(name="ring", bufs=4))
+        psum = ctx.enter_context(tc.psum_pool(name="psum", bufs=2))
+
+        offsets = keep.tile([P, S // 16], U16, name="offsets")
+        xw = keep.tile([P, T], I32, name="xw")
+        xs = keep.tile([P, T], U8, name="xs")
+        w1s = keep.tile([P, E, H], U8, name="w1s", align_bytes=64)
+        w3s = keep.tile([P, E, H], U8, name="w3s", align_bytes=64)
+        w2s = keep.tile([P, E, N], U8, name="w2s", align_bytes=64)
+        blank = keep.tile([P, P], F32, name="blank", tag="early", align_bytes=64)
+        ident = keep.tile([P, P], F32, name="ident")
+        zeros = [keep.tile([P, 8], F32, name="zero%d" % b, tag="late%d" % b, align_bytes=64) for b in range(3)]
+        wins = [keep.tile([P, T if b == 0 else WIDE], F32, name="win%d" % b) for b in range(3)]
+        ys = [keep.tile([P, S], F32, name="ys%d" % b) for b in range(3)]
+
+        nc.gpsimd.memset(xs[:].bitcast(I32), 0)
+        for b in range(3):
+            nc.vector.memset(zeros[b][:], 0.0)
+        nc.vector.memset(w1s[:].bitcast(I32), 0)
+        nc.vector.memset(w3s[:].bitcast(I32), 0)
+        nc.vector.memset(w2s[:].bitcast(I32), 0)
+        nc.gpsimd.memset(blank[:], 0.0)
+        nc.gpsimd.affine_select(
+            out=ident[:],
+            in_=blank[:],
+            pattern=[[-1, P]],
+            compare_op=mybir.AluOpType.not_equal,
+            fill=1.0,
+            base=0,
+            channel_multiplier=1,
+        )
+
+        def load_scale_rows(plane, scales, r):
+            rows = scales.rearrange("e s (q r) n -> r q (e s) n", r=4)[r]
+            nc.sync.dma_start(out=plane[r:P:32].bitcast(I32), in_=rows.bitcast(I32))
+
+        def load_words(tile, words, g):
+            src = words.rearrange("e s p b -> p (e s) b")[:, 2 * g : 2 * g + 2, :]
+            nc.sync.dma_start(out=tile.rearrange("p (e b) -> p e b", e=2).bitcast(I32), in_=src.bitcast(I32))
+
+        nc.sync.dma_start(offsets[:], offs)
+        nc.sync.dma_start(out=xw[:], in_=x_words.rearrange("o p t r -> p (o t r)").bitcast(I32))
+        for r in range(4):
+            rows = x_scales.rearrange("o (q r) t -> r q (o t)", r=4)[r]
+            nc.sync.dma_start(out=xs[r:P:32, :].bitcast(I32), in_=rows.bitcast(I32))
+        for r in range(4):
+            load_scale_rows(w1s, w1_scales, r)
+        for r in range(4):
+            load_scale_rows(w3s, w3_scales, r)
+        early = keep.tile([P, 8 * H], U8, name="early", tag="early", align_bytes=64)
+        load_words(early[:, : 4 * H], w1_words, 0)
+        load_words(early[:, 4 * H :], w3_words, 0)
+        for b in range(3):
+            nc.scalar.activation(out=wins[b][:, :T], in_=zeros[b][:, 0:1].to_broadcast([P, T]), func=RELU)
+        late = keep.tile([P, 8 * H + 2 * E * N], U8, name="late", tag="late0", align_bytes=64)
+        gates = keep.tile([P, S], F32, name="gates", tag="late2", align_bytes=64)
+        w1w = [early[:, : 4 * H], late[:, 0 : 4 * H]]
+        w3w = [early[:, 4 * H :], late[:, 4 * H : 8 * H]]
+        w2w = late[:, 8 * H :].rearrange("p (e b) -> p e b", e=E)
+        load_words(w1w[1], w1_words, 1)
+        load_words(w3w[1], w3_words, 1)
+        for r in range(4):
+            load_scale_rows(w2s, w2_scales, r)
+        nc.sync.dma_start(out=w2w.bitcast(I32), in_=w2_words.rearrange("e s p b -> p (e s) b").bitcast(I32))
+        nc.sync.dma_start(out=gates[:], in_=gate[0:P, :])
+
+        def offsets_of(e):
+            return offsets[:, e * (C // 16) : (e + 1) * (C // 16)]
+
+        gw0 = keep.tile([P, C], U32, name="gw0", align_bytes=64)
+        gw1 = keep.tile([P, S - C], U32, name="gw1", tag="late1", align_bytes=64)
+        gs0 = keep.tile([P, C], U8, name="gs0", align_bytes=64)
+        gs1 = keep.tile([P, S - C], U8, name="gs1", align_bytes=64)
+        gw = [gw0[:]] + [gw1[:, e * C : (e + 1) * C] for e in range(E - 1)]
+        gs = [gs0[:]] + [gs1[:, e * C : (e + 1) * C] for e in range(E - 1)]
+        nc.vector.tensor_copy(gw0[:], xw[:].bitcast(U32).indirect(offsets_of(0)))
+        nc.vector.tensor_copy(gs0[:], xs[:].indirect(offsets_of(0)))
+        nc.vector.tensor_copy(gs1[:], xs[:].indirect(offsets[:, C // 16 :]))
+        nc.vector.tensor_copy(gw1[:, :C], xw[:].bitcast(U32).indirect(offsets_of(1)))
+        nc.vector.tensor_copy(gw1[:, C:], xw[:].bitcast(U32).indirect(offsets[:, C // 8 :]))
+
+        def hidden(e, j):
+            cols = slice(j * P, (j + 1) * P)
+            a = psum.tile([P, H], F32, name="a")
+            b = psum.tile([P, H], F32, name="b")
+            for acc, words, plane in ((a, w1w, w1s), (b, w3w, w3s)):
+                nc.tensor.matmul_mx(
+                    out=acc[:],
+                    lhsT=gw[e][:, cols].bitcast(FP8X4),
+                    lhsT_scale=gs[e][:, cols],
+                    rhs=words[e // 2][:, (e % 2) * 2 * H : (e % 2 + 1) * 2 * H].bitcast(FP4X4),
+                    rhs_scale=plane[:, e, :],
+                    start=True,
+                    stop=True,
+                )
+            ra = ring.tile([P, 2, P, 2], F32, name="ra")
+            nc.scalar.activation(out=ra[:], in_=a[:].rearrange("s (p u d) -> s u p d", u=2, d=2), func=RELU)
+            h = ring.tile([P, H], BF16, name="h")
+            nc.vector.tensor_tensor(
+                h[:].rearrange("s (u p d) -> s u p d", u=2, d=2),
+                b[:].rearrange("s (p u d) -> s u p d", u=2, d=2),
+                ra[:],
+                MULT,
+            )
+            return h
+
+        def turn(hs):
+            turned = psum.tile([P, 2, 2, P], F32, name="turned")
+            for j in range(2):
+                pairs = hs[j][:].bitcast(F32)
+                for u in range(2):
+                    nc.tensor.transpose(turned[:, j, u, :], pairs[:, u * P : (u + 1) * P], ident[:])
+            ht = ring.tile([P, 4 * C], BF16, name="ht", align_bytes=64)
+            nc.scalar.copy(
+                out=ht[:].bitcast(F32).rearrange("p (j s u) -> p j s u", j=2, u=2),
+                in_=turned[:].rearrange("p j u s -> p j s u"),
+            )
+            return ht
+
+        def second(e, ht):
+            codes = ring.tile([P, C], U32, name="codes", align_bytes=64)
+            scales = ring.tile([P, C], U8, name="hscales", align_bytes=64)
+            nc.vector.quantize_mx(out=codes[:].bitcast(FP8X4), scales=scales[:], in_=ht[:])
+            for b in range(3):
+                y = psum.tile([P, C], F32, name="y")
+                nc.tensor.matmul_mx(
+                    out=y[:],
+                    lhsT=w2w[:, e, 2 * P * b : 2 * P * (b + 1)].bitcast(FP4X4),
+                    lhsT_scale=w2s[:, e, P * b : P * (b + 1)],
+                    rhs=codes[:].bitcast(FP8X4),
+                    rhs_scale=scales[:],
+                    start=True,
+                    stop=True,
+                )
+                nc.scalar.copy(out=ys[b][:, e * C : (e + 1) * C], in_=y[:])
+
+        def scatter_first(e):
+            cols = slice(e * C, (e + 1) * C)
+            nc.vector.tensor_tensor(wins[0][:].indirect(offsets_of(e)), ys[0][:, cols], gates[:, cols], MULT)
+
+        hs = {}
+        hts = {}
+        for step in range(E + 3):
+            if step < E:
+                hs[step] = [hidden(step, j) for j in range(2)]
+            if 1 <= step < E + 1:
+                hts[step - 1] = turn(hs[step - 1])
+            if 2 <= step < E + 2:
+                second(step - 2, hts[step - 2])
+            if step >= 3:
+                scatter_first(step - 3)
+        nc.sync.dma_start(out=out[0:P, :], in_=wins[0][:])
+        for b in (1, 2):
+            nc.vector.tensor_tensor(wins[b][:].indirect(offsets[:]), ys[b][:], gates[:], MULT)
+            nc.sync.dma_start(out=out[b * P : (b + 1) * P, :], in_=wins[b][:, :T])

@@ -39,8 +39,7 @@ def tile_moe_pkd_glu_relu_kernel(
         blank = keep.tile([P, P], F32, name="blank", tag="early", align_bytes=64)
         ident = keep.tile([P, P], F32, name="ident")
         zeros = [keep.tile([P, 8], F32, name="zero%d" % b, tag="late%d" % b, align_bytes=64) for b in range(3)]
-        wins = [keep.tile([P, T if b == 0 else WIDE], F32, name="win%d" % b) for b in range(3)]
-        ys = [keep.tile([P, S], F32, name="ys%d" % b) for b in range(3)]
+        wins = [keep.tile([P, T if b < 2 else WIDE], F32, name="win%d" % b) for b in range(3)]
 
         nc.gpsimd.memset(xs[:].bitcast(I32), 0)
         for b in range(3):
@@ -93,25 +92,22 @@ def tile_moe_pkd_glu_relu_kernel(
         nc.sync.dma_start(out=w2w.bitcast(I32), in_=w2_words.rearrange("e s p b -> p (e s) b").bitcast(I32))
         nc.sync.dma_start(out=gates[:], in_=gate[0:P, :])
 
-        def offsets_of(e):
-            return offsets[:, e * (C // 16) : (e + 1) * (C // 16)]
+        def gather(out_ap, window, lo, hi):
+            nc.vector.tensor_copy(out_ap, window.indirect(offsets[:, lo // 16 : hi // 16]))
 
-        gw0 = keep.tile([P, C], U32, name="gw0", align_bytes=64)
-        gw1 = keep.tile([P, S - C], U32, name="gw1", tag="late1", align_bytes=64)
-        gs0 = keep.tile([P, C], U8, name="gs0", align_bytes=64)
-        gs1 = keep.tile([P, S - C], U8, name="gs1", align_bytes=64)
-        gw = [gw0[:]] + [gw1[:, e * C : (e + 1) * C] for e in range(E - 1)]
-        gs = [gs0[:]] + [gs1[:, e * C : (e + 1) * C] for e in range(E - 1)]
-        nc.vector.tensor_copy(gw0[:], xw[:].bitcast(U32).indirect(offsets_of(0)))
-        nc.vector.tensor_copy(gs0[:], xs[:].indirect(offsets_of(0)))
-        nc.vector.tensor_copy(gs1[:], xs[:].indirect(offsets[:, C // 16 :]))
-        nc.vector.tensor_copy(gw1[:, :C], xw[:].bitcast(U32).indirect(offsets_of(1)))
-        nc.vector.tensor_copy(gw1[:, C:], xw[:].bitcast(U32).indirect(offsets[:, C // 8 :]))
+        gw_first = keep.tile([P, 3 * C], U32, name="gw_first", align_bytes=64)
+        gs_first = keep.tile([P, 3 * C], U8, name="gs_first", align_bytes=64)
+        for lo, hi in ((0, 2 * C), (2 * C, 3 * C)):
+            gather(gw_first[:, lo:hi], xw[:].bitcast(U32), lo, hi)
+        for e in range(3):
+            gather(gs_first[:, e * C : (e + 1) * C], xs[:], e * C, (e + 1) * C)
+        gw = [gw_first[:, e * C : (e + 1) * C] for e in range(3)]
+        gs = [gs_first[:, e * C : (e + 1) * C] for e in range(3)]
 
         def hidden(e, j):
             cols = slice(j * P, (j + 1) * P)
             a = psum.tile([P, H], F32, name="a")
-            b = psum.tile([P, H], F32, name="b")
+            b = psum.tile([P, H], F32, name="b", bufs=3)
             for acc, words, plane in ((a, w1w, w1s), (b, w3w, w3s)):
                 nc.tensor.matmul_mx(
                     out=acc[:],
@@ -122,9 +118,9 @@ def tile_moe_pkd_glu_relu_kernel(
                     start=True,
                     stop=True,
                 )
-            ra = ring.tile([P, 2, P, 2], F32, name="ra")
+            ra = keep.tile([P, 2, P, 2], F32, name="ra", tag="ra%d%d" % (e, j), align_bytes=64)
             nc.scalar.activation(out=ra[:], in_=a[:].rearrange("s (p u d) -> s u p d", u=2, d=2), func=RELU)
-            h = ring.tile([P, H], BF16, name="h")
+            h = keep.tile([P, H], BF16, name="h", tag="h%d%d" % (e, j), align_bytes=64)
             nc.vector.tensor_tensor(
                 h[:].rearrange("s (u p d) -> s u p d", u=2, d=2),
                 b[:].rearrange("s (p u d) -> s u p d", u=2, d=2),
@@ -133,52 +129,75 @@ def tile_moe_pkd_glu_relu_kernel(
             )
             return h
 
-        def turn(hs):
-            turned = psum.tile([P, 2, 2, P], F32, name="turned")
+        def turn(e, hs):
+            turned = psum.tile([P, 2, 2, P], F32, name="turned", bufs=1)
             for j in range(2):
                 pairs = hs[j][:].bitcast(F32)
                 for u in range(2):
                     nc.tensor.transpose(turned[:, j, u, :], pairs[:, u * P : (u + 1) * P], ident[:])
-            ht = ring.tile([P, 4 * C], BF16, name="ht", align_bytes=64)
+            ht = keep.tile([P, 4 * C], BF16, name="ht", tag="ht%d" % e, align_bytes=64)
             nc.scalar.copy(
                 out=ht[:].bitcast(F32).rearrange("p (j s u) -> p j s u", j=2, u=2),
                 in_=turned[:].rearrange("p j u s -> p j s u"),
             )
             return ht
 
-        def second(e, ht):
-            codes = ring.tile([P, C], U32, name="codes", align_bytes=64)
-            scales = ring.tile([P, C], U8, name="hscales", align_bytes=64)
+        def quantise(e, ht):
+            codes = keep.tile([P, C], U32, name="codes%d" % e, align_bytes=64)
+            scales = keep.tile([P, C], U8, name="hscales%d" % e, align_bytes=64)
             nc.vector.quantize_mx(out=codes[:].bitcast(FP8X4), scales=scales[:], in_=ht[:])
-            for b in range(3):
-                y = psum.tile([P, C], F32, name="y")
-                nc.tensor.matmul_mx(
-                    out=y[:],
-                    lhsT=w2w[:, e, 2 * P * b : 2 * P * (b + 1)].bitcast(FP4X4),
-                    lhsT_scale=w2s[:, e, P * b : P * (b + 1)],
-                    rhs=codes[:].bitcast(FP8X4),
-                    rhs_scale=scales[:],
-                    start=True,
-                    stop=True,
-                )
-                nc.scalar.copy(out=ys[b][:, e * C : (e + 1) * C], in_=y[:])
+            return codes, scales
 
-        def scatter_first(e):
-            cols = slice(e * C, (e + 1) * C)
-            nc.vector.tensor_tensor(wins[0][:].indirect(offsets_of(e)), ys[0][:, cols], gates[:, cols], MULT)
+        def second(y, e, b):
+            codes, scales = hq[e]
+            nc.tensor.matmul_mx(
+                out=y,
+                lhsT=w2w[:, e, 2 * P * b : 2 * P * (b + 1)].bitcast(FP4X4),
+                lhsT_scale=w2s[:, e, P * b : P * (b + 1)],
+                rhs=codes[:].bitcast(FP8X4),
+                rhs_scale=scales[:],
+                start=True,
+                stop=True,
+            )
 
-        hs = {}
-        hts = {}
-        for step in range(E + 3):
-            if step < E:
-                hs[step] = [hidden(step, j) for j in range(2)]
-            if 1 <= step < E + 1:
-                hts[step - 1] = turn(hs[step - 1])
-            if 2 <= step < E + 2:
-                second(step - 2, hts[step - 2])
-            if step >= 3:
-                scatter_first(step - 3)
-        nc.sync.dma_start(out=out[0:P, :], in_=wins[0][:])
-        for b in (1, 2):
-            nc.vector.tensor_tensor(wins[b][:].indirect(offsets[:]), ys[b][:], gates[:], MULT)
-            nc.sync.dma_start(out=out[b * P : (b + 1) * P, :], in_=wins[b][:, :T])
+        def scatter(b, lo, hi, ys):
+            nc.vector.tensor_tensor(wins[b][:].indirect(offsets[:, lo // 16 : hi // 16]), ys, gates[:, lo:hi], MULT)
+
+        def single(e, b, tag):
+            y = psum.tile([P, C], F32, name="y")
+            second(y[:], e, b)
+            ys = keep.tile([P, C], F32, name="ys", tag=tag, align_bytes=64)
+            nc.scalar.copy(out=ys[:], in_=y[:])
+            scatter(b, e * C, (e + 1) * C, ys[:])
+
+        def pair(g, b, ys):
+            y = psum.tile([P, 2 * C], F32, name="pair", tag="a")
+            for j in range(2):
+                second(y[:, j * C : (j + 1) * C], 2 * g + j, b)
+            nc.scalar.copy(out=ys, in_=y[:])
+
+        hq = {}
+        for e in range(E):
+            ht = turn(e, [hidden(e, j) for j in range(2)])
+            hq[e] = quantise(e, ht)
+            if e == 1:
+                gs_last = keep.tile([P, C], U8, name="gs_last", tag="ra10", align_bytes=64)
+                gw_last = keep.tile([P, C], U32, name="gw_last", tag="ra11", align_bytes=64)
+                gather(gs_last[:], xs[:], 3 * C, S)
+                gather(gw_last[:], xw[:].bitcast(U32), 3 * C, S)
+                gs.append(gs_last[:])
+                gw.append(gw_last[:])
+            if e >= 2:
+                single(0, e - 2, "ra%d1" % e)
+        single(1, 0, "h31")
+        single(1, 1, "h30")
+        for b in range(2):
+            ys = keep.tile([P, 2 * C], F32, name="ys%d" % b)
+            pair(1, b, ys[:])
+            scatter(b, 2 * C, S, ys[:])
+            nc.sync.dma_start(out=out[b * P : (b + 1) * P, :], in_=wins[b][:])
+        ys = keep.tile([P, S], F32, name="ys2")
+        for g in range(2):
+            pair(g, 2, ys[:, 2 * g * C : 2 * (g + 1) * C])
+        scatter(2, 0, S, ys[:])
+        nc.sync.dma_start(out=out[2 * P :, :], in_=wins[2][:, :T])

from contextlib import ExitStack

import concourse.mybir as mybir

K, T, E, C, H, N = 512, 1280, 4, 256, 512, 384
S = E * C
P = 128
FLOPS = 2 * S * (2 * K * H + H * N)

F32 = mybir.dt.float32
BF16 = mybir.dt.bfloat16
I32 = mybir.dt.int32
U32 = mybir.dt.uint32
U16 = mybir.dt.uint16
U8 = mybir.dt.uint8
FP8X4 = mybir.dt.float8_e4m3fn_x4
FP4X4 = mybir.dt.float4_e2m1fn_x4
MULT = mybir.AluOpType.mult
RELU = mybir.ActivationFunctionType.Relu

WIDE = 1376


def tile_moe_pkd_glu_relu_kernel(
    tc, x_words, x_scales, w1_words, w1_scales, w3_words, w3_scales, w2_words, w2_scales, gate, offs, out
):
    nc = tc.nc
    with ExitStack() as ctx:
        keep = ctx.enter_context(tc.tile_pool(name="keep", bufs=1))
        ring = ctx.enter_context(tc.tile_pool(name="ring", bufs=4))
        psum = ctx.enter_context(tc.psum_pool(name="psum", bufs=2))

        offsets = keep.tile([P, S // 16], U16, name="offsets")
        xw = keep.tile([P, T], I32, name="xw")
        xs = keep.tile([P, T], U8, name="xs")
        w1s = keep.tile([P, E, H], U8, name="w1s", align_bytes=64)
        w3s = keep.tile([P, E, H], U8, name="w3s", align_bytes=64)
        w2s = keep.tile([P, E, N], U8, name="w2s", align_bytes=64)
        blank = keep.tile([P, P], F32, name="blank", tag="early", align_bytes=64)
        ident = keep.tile([P, P], F32, name="ident")
        zeros = [keep.tile([P, 8], F32, name="zero%d" % b, tag="late%d" % b, align_bytes=64) for b in range(3)]
        wins = [keep.tile([P, T if b < 2 else WIDE], F32, name="win%d" % b) for b in range(3)]

        nc.gpsimd.memset(xs[:].bitcast(I32), 0)
        for b in range(3):
            nc.vector.memset(zeros[b][:], 0.0)
        nc.vector.memset(w1s[:].bitcast(I32), 0)
        nc.vector.memset(w3s[:].bitcast(I32), 0)
        nc.vector.memset(w2s[:].bitcast(I32), 0)
        nc.gpsimd.memset(blank[:], 0.0)
        nc.gpsimd.affine_select(
            out=ident[:],
            in_=blank[:],
            pattern=[[-1, P]],
            compare_op=mybir.AluOpType.not_equal,
            fill=1.0,
            base=0,
            channel_multiplier=1,
        )

        def load_scale_rows(plane, scales, r):
            rows = scales.rearrange("e s (q r) n -> r q (e s) n", r=4)[r]
            nc.sync.dma_start(out=plane[r:P:32].bitcast(I32), in_=rows.bitcast(I32))

        def load_words(tile, words, g):
            src = words.rearrange("e s p b -> p (e s) b")[:, 2 * g : 2 * g + 2, :]
            nc.sync.dma_start(out=tile.rearrange("p (e b) -> p e b", e=2).bitcast(I32), in_=src.bitcast(I32))

        nc.sync.dma_start(offsets[:], offs)
        nc.sync.dma_start(out=xw[:], in_=x_words.rearrange("o p t r -> p (o t r)").bitcast(I32))
        for r in range(4):
            rows = x_scales.rearrange("o (q r) t -> r q (o t)", r=4)[r]
            nc.sync.dma_start(out=xs[r:P:32, :].bitcast(I32), in_=rows.bitcast(I32))
        for r in range(4):
            load_scale_rows(w1s, w1_scales, r)
        for r in range(4):
            load_scale_rows(w3s, w3_scales, r)
        early = keep.tile([P, 8 * H], U8, name="early", tag="early", align_bytes=64)
        load_words(early[:, : 4 * H], w1_words, 0)
        load_words(early[:, 4 * H :], w3_words, 0)
        for b in range(3):
            nc.scalar.activation(out=wins[b][:, :T], in_=zeros[b][:, 0:1].to_broadcast([P, T]), func=RELU)
        late = keep.tile([P, 8 * H + 2 * E * N], U8, name="late", tag="late0", align_bytes=64)
        gates = keep.tile([P, S], F32, name="gates", tag="late2", align_bytes=64)
        w1w = [early[:, : 4 * H], late[:, 0 : 4 * H]]
        w3w = [early[:, 4 * H :], late[:, 4 * H : 8 * H]]
        w2w = late[:, 8 * H :].rearrange("p (e b) -> p e b", e=E)
        load_words(w1w[1], w1_words, 1)
        load_words(w3w[1], w3_words, 1)
        for r in range(4):
            load_scale_rows(w2s, w2_scales, r)
        nc.sync.dma_start(out=w2w.bitcast(I32), in_=w2_words.rearrange("e s p b -> p (e s) b").bitcast(I32))
        nc.sync.dma_start(out=gates[:], in_=gate[0:P, :])

        def gather(out_ap, window, lo, hi):
            nc.vector.tensor_copy(out_ap, window.indirect(offsets[:, lo // 16 : hi // 16]))

        gw_first = keep.tile([P, 3 * C], U32, name="gw_first", align_bytes=64)
        gs_first = keep.tile([P, 3 * C], U8, name="gs_first", align_bytes=64)
        for lo, hi in ((0, 2 * C), (2 * C, 3 * C)):
            gather(gw_first[:, lo:hi], xw[:].bitcast(U32), lo, hi)
        for e in range(3):
            gather(gs_first[:, e * C : (e + 1) * C], xs[:], e * C, (e + 1) * C)
        gw = [gw_first[:, e * C : (e + 1) * C] for e in range(3)]
        gs = [gs_first[:, e * C : (e + 1) * C] for e in range(3)]

        def hidden(e, j):
            cols = slice(j * P, (j + 1) * P)
            a = psum.tile([P, H], F32, name="a")
            b = psum.tile([P, H], F32, name="b", bufs=3)
            for acc, words, plane in ((a, w1w, w1s), (b, w3w, w3s)):
                nc.tensor.matmul_mx(
                    out=acc[:],
                    lhsT=gw[e][:, cols].bitcast(FP8X4),
                    lhsT_scale=gs[e][:, cols],
                    rhs=words[e // 2][:, (e % 2) * 2 * H : (e % 2 + 1) * 2 * H].bitcast(FP4X4),
                    rhs_scale=plane[:, e, :],
                    start=True,
                    stop=True,
                )
            ra = keep.tile([P, 2, P, 2], F32, name="ra", tag="ra%d%d" % (e, j), align_bytes=64)
            nc.scalar.activation(out=ra[:], in_=a[:].rearrange("s (p u d) -> s u p d", u=2, d=2), func=RELU)
            h = keep.tile([P, H], BF16, name="h", tag="h%d%d" % (e, j), align_bytes=64)
            nc.vector.tensor_tensor(
                h[:].rearrange("s (u p d) -> s u p d", u=2, d=2),
                b[:].rearrange("s (p u d) -> s u p d", u=2, d=2),
                ra[:],
                MULT,
            )
            return h

        def turn(e, hs):
            turned = psum.tile([P, 2, 2, P], F32, name="turned", bufs=1)
            for j in range(2):
                pairs = hs[j][:].bitcast(F32)
                for u in range(2):
                    nc.tensor.transpose(turned[:, j, u, :], pairs[:, u * P : (u + 1) * P], ident[:])
            ht = keep.tile([P, 4 * C], BF16, name="ht", tag="ht%d" % e, align_bytes=64)
            nc.scalar.copy(
                out=ht[:].bitcast(F32).rearrange("p (j s u) -> p j s u", j=2, u=2),
                in_=turned[:].rearrange("p j u s -> p j s u"),
            )
            return ht

        def quantise(e, ht):
            codes = keep.tile([P, C], U32, name="codes%d" % e, align_bytes=64)
            scales = keep.tile([P, C], U8, name="hscales%d" % e, align_bytes=64)
            nc.vector.quantize_mx(out=codes[:].bitcast(FP8X4), scales=scales[:], in_=ht[:])
            return codes, scales

        def second(y, e, b):
            codes, scales = hq[e]
            nc.tensor.matmul_mx(
                out=y,
                lhsT=w2w[:, e, 2 * P * b : 2 * P * (b + 1)].bitcast(FP4X4),
                lhsT_scale=w2s[:, e, P * b : P * (b + 1)],
                rhs=codes[:].bitcast(FP8X4),
                rhs_scale=scales[:],
                start=True,
                stop=True,
            )

        def scatter(b, lo, hi, ys):
            nc.vector.tensor_tensor(wins[b][:].indirect(offsets[:, lo // 16 : hi // 16]), ys, gates[:, lo:hi], MULT)

        def single(e, b, tag):
            y = psum.tile([P, C], F32, name="y")
            second(y[:], e, b)
            ys = keep.tile([P, C], F32, name="ys", tag=tag, align_bytes=64)
            nc.scalar.copy(out=ys[:], in_=y[:])
            scatter(b, e * C, (e + 1) * C, ys[:])

        def pair(g, b, ys):
            y = psum.tile([P, 2 * C], F32, name="pair", tag="a")
            for j in range(2):
                second(y[:, j * C : (j + 1) * C], 2 * g + j, b)
            nc.scalar.copy(out=ys, in_=y[:])

        hq = {}
        for e in range(E):
            ht = turn(e, [hidden(e, j) for j in range(2)])
            hq[e] = quantise(e, ht)
            if e == 1:
                gs_last = keep.tile([P, C], U8, name="gs_last", tag="ra10", align_bytes=64)
                gw_last = keep.tile([P, C], U32, name="gw_last", tag="ra11", align_bytes=64)
                gather(gs_last[:], xs[:], 3 * C, S)
                gather(gw_last[:], xw[:].bitcast(U32), 3 * C, S)
                gs.append(gs_last[:])
                gw.append(gw_last[:])
            if e >= 2:
                single(0, e - 2, "ra%d1" % e)
        single(1, 0, "h31")
        single(1, 1, "h30")
        for b in range(2):
            ys = keep.tile([P, 2 * C], F32, name="ys%d" % b)
            pair(1, b, ys[:])
            scatter(b, 2 * C, S, ys[:])
            nc.sync.dma_start(out=out[b * P : (b + 1) * P, :], in_=wins[b][:])
        ys = keep.tile([P, S], F32, name="ys2")
        for g in range(2):
            pair(g, 2, ys[:, 2 * g * C : 2 * (g + 1) * C])
        scatter(2, 0, S, ys[:])
        nc.sync.dma_start(out=out[2 * P :, :], in_=wins[2][:, :T])
